import numpy as np
import ml_dtypes


def mxq(x, axis, fmt="e4m3"):
    dtype, down = {"e4m3": (ml_dtypes.float8_e4m3fn, 7), "e5m2": (ml_dtypes.float8_e5m2, 14)}[fmt]
    v = np.moveaxis(np.asarray(x, np.float32).astype(ml_dtypes.bfloat16).astype(np.float64), axis, -1)
    blocks = v.reshape(v.shape[:-1] + (-1, 32))
    amax = np.abs(blocks).max(-1, keepdims=True)
    byte = np.maximum(np.where(amax > 0, np.frexp(amax)[1] - 1 + 127, 0) - down, 1)
    scale = np.exp2(byte - 127.0)
    codes = (blocks / scale).astype(np.float32).astype(dtype).astype(np.float64)
    return np.moveaxis((codes * scale).reshape(v.shape), -1, axis)


WIDE = False


def mx_kscale(k):
    if not WIDE:
        return np.ones(k)
    levels = np.array([10, -10, 5, -5, 0])
    if k % 512:
        return np.exp2(np.random.permutation(np.resize(levels, k // 32))).repeat(32)
    a = np.empty((k // 512, 16))
    for p in range(k // 512):
        a[p, :8] = np.random.permutation(np.resize(levels, 8))
        for g in range(8):
            far = levels[np.abs(levels - a[p, g]) >= 10]
            a[p, g + 8] = far[np.random.randint(len(far))]
    return np.exp2(a.ravel()).repeat(32)


BF16 = ml_dtypes.bfloat16


def bf(x):
    return np.asarray(x, np.float32).astype(BF16)


def f64(x):
    return np.asarray(x).astype(np.float64)


E2M1 = np.array([0.0, 0.5, 1.0, 1.5, 2.0, 3.0, 4.0, 6.0, -0.0, -0.5, -1.0, -1.5, -2.0, -3.0, -4.0, -6.0])


def pack_weight(w, fmt):
    k, n = w.shape
    w = f64(bf(w)).reshape(k // 32, 32, n)
    amax = np.abs(w).max(1)
    if fmt == "e4m3":
        byte = np.frexp(amax)[1] - 1 + 127 - 7
    else:
        mant, ex = np.frexp(amax / 6.0)
        byte = np.where(mant > 0.5, ex, ex - 1) + 127
    byte = np.clip(np.where(amax > 0, byte, 1), 1, 254)
    scaled = (w * np.exp2(127.0 - byte)[:, None, :]).reshape(k, n).astype(np.float32)
    by_word = np.ascontiguousarray(scaled.reshape(k // 512, 128, 4, n).transpose(0, 1, 3, 2))
    if fmt == "e4m3":
        words = by_word.astype(ml_dtypes.float8_e4m3fn).view(np.uint8)
    else:
        c = by_word.astype(ml_dtypes.float4_e2m1fn).view(np.uint8) & 0xF
        words = c[..., 0::2] | (c[..., 1::2] << 4)
    return np.ascontiguousarray(words), np.ascontiguousarray(byte.astype(np.uint8).reshape(k // 512, 16, n))


def unpack_weight(words, scales, fmt):
    g, p, n, _ = words.shape
    if fmt == "e4m3":
        vals = np.ascontiguousarray(words).view(ml_dtypes.float8_e4m3fn).astype(np.float64)
    else:
        nib = np.empty((g, p, n, 4), np.uint8)
        nib[..., 0::2] = words & 0xF
        nib[..., 1::2] = words >> 4
        vals = E2M1[nib]
    vals = vals * np.repeat(np.exp2(scales.astype(np.float64) - 127.0), 8, axis=1)[..., None]
    return vals.transpose(0, 1, 3, 2).reshape(g * 512, n)
def pack4(w):
    words, scales = pack_weight(w, "e2m1")
    return words.reshape(words.shape[0], 128, -1), scales


def unpack4(words, scales):
    return unpack_weight(words.reshape(words.shape[0], 128, -1, 2), scales, "e2m1")


def planes(Y):
    n, m = Y.shape
    b = f64(bf(Y)).reshape(n // 32, 32, m)
    amax = np.abs(b).max(1)
    byte = np.clip(np.where(amax > 0, np.frexp(amax)[1] - 1 + 127 - 7, 1), 1, 254)
    codes = (b * np.exp2(127.0 - byte)[:, None, :]).reshape(n, m).astype(np.float32).astype(ml_dtypes.float8_e4m3fn).view(np.uint8)
    words = codes.reshape(n // 512, 128, 4, m).transpose(0, 1, 3, 2)
    return np.ascontiguousarray(words), np.ascontiguousarray(byte.astype(np.uint8).reshape(n // 512, 16, m))


M, KQ, KV, N = 1024, 1024, 2048, 1536
WEIGHT_GAIN = 1.2
GAIN_SPREAD = 0.8

def setup_inputs():
    sq = mx_kscale(KQ)
    sv = mx_kscale(KV)
    question = np.random.randn(M, KQ) * sq[None, :]
    image = np.random.randn(M, KV) * sv[None, :]
    wq = WEIGHT_GAIN * np.random.randn(KQ, N) / np.sqrt(KQ) / sq[:, None]
    wv = WEIGHT_GAIN * np.random.randn(KV, N) / np.sqrt(KV) / sv[:, None]
    wq_words, wq_scales = pack4(wq)
    wv_words, wv_scales = pack4(wv)
    joint_gain = np.exp(GAIN_SPREAD * np.random.randn(N))
    return {"question": bf(question), "image": bf(image),
            "wq_words": wq_words, "wq_scales": wq_scales,
            "wv_words": wv_words, "wv_scales": wv_scales,
            "joint_gain": bf(joint_gain)}

def reference(question, image, wq_words, wq_scales, wv_words, wv_scales, joint_gain):
    a = mxq(f64(question), 1, "e4m3") @ unpack4(wq_words, wq_scales)
    b = mxq(f64(image), 1, "e4m3") @ unpack4(wv_words, wv_scales)
    y = np.tanh(a) * np.tanh(b) * f64(joint_gain)[None, :]
    Y = y.T
    words, scales = planes(Y)
    return y, words, scales

@@ -1,0 +1,286 @@
+from contextlib import ExitStack
+
+import concourse.mybir as mybir
+from concourse.masks import make_identity
+
+M, KQ, KV, N = 1024, 1024, 2048, 1536
+FLOPS = 2 * M * (KQ + KV) * N
+
+F32 = mybir.dt.float32
+BF16 = mybir.dt.bfloat16
+I32 = mybir.dt.int32
+U32 = mybir.dt.uint32
+U8 = mybir.dt.uint8
+FP8X4 = mybir.dt.float8_e4m3fn_x4
+FP4X4 = mybir.dt.float4_e2m1fn_x4
+TANH = mybir.ActivationFunctionType.Tanh
+MULT = mybir.AluOpType.mult
+
+P = 128
+K_PASS = 512
+N_TILE = 512
+GQ = KQ // K_PASS
+GV = KV // K_PASS
+G = GQ + GV
+M_TILES = M // P
+N_TILES = N // N_TILE
+ACC_BANKS = 4
+TR_BANKS = 4
+
+
+def tile_question_image_joint_features_g4_kernel(
+    tc, question, image, wq_words, wq_scales, wv_words, wv_scales, joint_gain, out_0, out_1, out_2
+):
+    nc = tc.nc
+    with ExitStack() as ctx:
+        keep = ctx.enter_context(tc.tile_pool(name="keep", bufs=1))
+        work = ctx.enter_context(tc.tile_pool(name="work", bufs=3))
+        psum = ctx.enter_context(tc.psum_pool(name="psum", bufs=1))
+        ctx.enter_context(tc.manual_schedule())
+
+        counters = {"acc": 0, "tr": 0}
+
+        def next_bank(kind, banks, shape):
+            name = "%s%d" % (kind, counters[kind] % banks)
+            counters[kind] = counters[kind] + 1
+            return psum.tile(shape, F32, name=name, tag=name)
+
+        ident = keep.tile([P, P], F32, name="ident", align_bytes=64)
+        warm_in = keep.tile([P, 8], F32, name="warm_in")
+        warm_out = keep.tile([P, 8], F32, name="warm_out")
+        gain_rows = keep.tile([P, N_TILES, 4], BF16, name="gain_rows")
+        gain = keep.tile([P, N], BF16, name="gain", align_bytes=64)
+        xq = [keep.tile([P, KQ], BF16, name="xq%d" % m, align_bytes=64) for m in range(M_TILES)]
+        xv = [keep.tile([P, KV], BF16, name="xv%d" % m, align_bytes=64) for m in range(M_TILES)]
+        wq = [keep.tile([P, GQ, 2 * N_TILE], U8, name="wq%d" % n, align_bytes=64) for n in range(N_TILES)]
+        wv = [keep.tile([P, GV, 2 * N_TILE], U8, name="wv%d" % n, align_bytes=64) for n in range(N_TILES)]
+        sq = keep.tile([P, GQ, N], U8, name="sq", align_bytes=64)
+        sv_first = keep.tile([P, GV, N_TILE], U8, name="sv_first", align_bytes=64)
+        sv_rest = keep.tile([P, GV, N - N_TILE], U8, name="sv_rest", align_bytes=64)
+        groups = [(0, 4), (4, 7), (7, 8)]
+        y_codes = [keep.tile([P, N_TILES, (b - a) * P], U32, name="y_codes%d" % a, align_bytes=64) for a, b in groups]
+        y_scales_main = keep.tile([P, N_TILES, 7 * P], U8, name="y_scales_main", align_bytes=64)
+        y_scales_last = keep.tile([P, N_TILES, P], U8, name="y_scales_last", align_bytes=64)
+
+        def load_x(m):
+            rows = slice(m * P, (m + 1) * P)
+            nc.sync.dma_start(out=xq[m][:], in_=question[rows, :])
+            nc.sync.dma_start(out=xv[m][:], in_=image[rows, :])
+
+        def load_words(tile, words, n):
+            src = words[:, :, 2 * N_TILE * n : 2 * N_TILE * (n + 1)].rearrange("g p b -> p g b")
+            nc.sync.dma_start(out=tile[:].bitcast(I32), in_=src.bitcast(I32))
+
+        def load_scales(tile, scales, cols):
+            for q in range(4):
+                src = scales[:, 4 * q : 4 * q + 4, cols].rearrange("g r n -> r g n")
+                nc.sync.dma_start(out=tile[32 * q : 32 * q + 4].bitcast(I32), in_=src.bitcast(I32))
+
+        x_codes = {}
+        x_scales = {}
+
+        def turn_x(m):
+            codes = work.tile([P, G * P], U32, name="x_codes", align_bytes=64)
+            scales = work.tile([P, G * P], U8, name="x_scales", align_bytes=64)
+            x_codes[m] = codes
+            x_scales[m] = scales
+            for pair in range(G // 2):
+                src = xq[m] if pair == 0 else xv[m]
+                first = 0 if pair == 0 else (pair - 1) * 2
+                words = src[:].bitcast(F32)
+                bank = next_bank("tr", TR_BANKS, [P, 4, P])
+                for gl in range(2):
+                    g = first + gl
+                    for u in range(2):
+                        nc.tensor.transpose(bank[:, 2 * gl + u, :], words[:, 256 * g + u : 256 * (g + 1) : 2], ident[:])
+                xt = work.tile([P, 2 * K_PASS], BF16, name="xt", align_bytes=64)
+                nc.scalar.copy(
+                    out=xt[:].bitcast(F32).rearrange("p (g m u) -> p g m u", g=2, u=2),
+                    in_=bank[:].rearrange("p (g u) m -> p g m u", u=2),
+                )
+                cols = slice(2 * P * pair, 2 * P * (pair + 1))
+                nc.vector.quantize_mx(out=codes[:, cols].bitcast(FP8X4), scales=scales[:, cols], in_=xt[:])
+
+        def w_scale(is_q, g, n):
+            if is_q:
+                return sq[:, g, n * N_TILE : (n + 1) * N_TILE]
+            if n == 0:
+                return sv_first[:, g, :]
+            return sv_rest[:, g, (n - 1) * N_TILE : n * N_TILE]
+
+        def project(m, n, is_q):
+            acc = next_bank("acc", ACC_BANKS, [P, N_TILE])
+            passes = GQ if is_q else GV
+            first = 0 if is_q else GQ
+            w = wq[n] if is_q else wv[n]
+            for g in range(passes):
+                cols = slice((first + g) * P, (first + g + 1) * P)
+                nc.tensor.matmul_mx(
+                    out=acc[:],
+                    lhsT=x_codes[m][:, cols].bitcast(FP8X4),
+                    lhsT_scale=x_scales[m][:, cols],
+                    rhs=w[:, g, :].bitcast(FP4X4),
+                    rhs_scale=w_scale(is_q, g, n),
+                    start=(g == 0),
+                    stop=(g == passes - 1),
+                )
+            th = work.tile([P, N_TILE], F32, name="tanh_q" if is_q else "tanh_v")
+            nc.scalar.activation(out=th[:], in_=acc[:], func=TANH)
+            return th
+
+        chunks = [(0, 0), (1, 0), (0, 1), (1, 1), (0, 2), (1, 2)]
+        chunks = chunks + [(m, n) for m in range(2, M_TILES) for n in range(N_TILES)]
+        last = len(chunks) - 1
+        gained = {}
+        y32 = {}
+        y16 = {}
+
+        def gain_mul(i, th):
+            n = chunks[i][1]
+            t = work.tile([P, N_TILE], F32, name="gained")
+            nc.vector.tensor_tensor(out=t[:], in0=th[:], in1=gain[:, n * N_TILE : (n + 1) * N_TILE], op=MULT)
+            gained[i] = t
+
+        def product(i, th):
+            m, n = chunks[i]
+            y = work.tile([P, N_TILE], F32, name="y32", bufs=5)
+            nc.vector.tensor_tensor(out=y[:], in0=gained[i][:], in1=th[:], op=MULT)
+            y32[i] = y
+            nc.sync.dma_start(out=out_0[m * P : (m + 1) * P, n * N_TILE : (n + 1) * N_TILE], in_=y[:])
+
+        def split_view(ap):
+            return ap.rearrange("p (q u e) -> p u q e", u=2, e=2)
+
+        def cast(i):
+            h = work.tile([P, N_TILE], BF16, name="y16", bufs=6, align_bytes=64)
+            nc.vector.tensor_copy(out=h[:].rearrange("p (u q e) -> p u q e", u=2, e=2), in_=split_view(y32[i][:]))
+            y16[i] = h
+
+        def turn_y(ids):
+            bank = next_bank("tr", TR_BANKS, [P, 4, P])
+            for c, i in enumerate(ids):
+                words = y16[i][:].bitcast(F32)
+                for u in range(2):
+                    nc.tensor.transpose(bank[:, 2 * c + u, :], words[:, u * P : (u + 1) * P], ident[:])
+            return bank
+
+        def drain_y(ids, bank):
+            count = len(ids)
+            yt = work.tile([P, 2 * N_TILE], BF16, name="yt", align_bytes=64)
+            nc.scalar.copy(
+                out=yt[:, : count * N_TILE].bitcast(F32).rearrange("p (c m u) -> p c m u", c=count, u=2),
+                in_=bank[:, : 2 * count, :].rearrange("p (c u) m -> p c m u", u=2),
+            )
+            return yt
+
+        def quantize_y(ids, yt):
+            for c, i in enumerate(ids):
+                m, n = chunks[i]
+                k = [j for j, (a, b) in enumerate(groups) if a <= m < b][0]
+                off = (m - groups[k][0]) * P
+                if m < M_TILES - 1:
+                    scales = y_scales_main[:, n, m * P : (m + 1) * P]
+                else:
+                    scales = y_scales_last[:, n, :]
+                nc.vector.quantize_mx(
+                    out=y_codes[k][:, n, off : off + P].bitcast(FP8X4),
+                    scales=scales,
+                    in_=yt[:, c * N_TILE : (c + 1) * N_TILE],
+                )
+
+        def store_codes(k, ns):
+            a, b = groups[k]
+            dst = out_1.rearrange("g p m t -> p g (m t)")[:, ns, 4 * P * a : 4 * P * b]
+            nc.sync.dma_start(out=dst.bitcast(I32), in_=y_codes[k][:, ns, :].bitcast(I32))
+
+        def store_scales(tile, cols, queues):
+            for q in range(4):
+                dst = out_2[:, 4 * q : 4 * q + 4, cols].rearrange("g r m -> r g m")
+                queues[q].dma_start(out=dst.bitcast(I32), in_=tile[32 * q : 32 * q + 4].bitcast(I32))
+
+        nc.sync.dma_start(out=gain_rows[:], in_=joint_gain.rearrange("(j p e) -> p j e", p=P, e=4))
+        load_x(0)
+        load_x(1)
+        nc.vector.memset(warm_in[:], 0.0)
+        nc.scalar.activation(out=warm_out[:], in_=warm_in[:], func=TANH)
+        make_identity(nc, ident[:])
+        for tile in (sq, sv_first, sv_rest):
+            nc.vector.memset(tile[:].rearrange("p g n -> p (g n)").bitcast(I32), 0)
+        load_scales(sq, wq_scales, slice(0, N))
+        load_words(wq[0], wq_words, 0)
+        load_scales(sv_first, wv_scales, slice(0, N_TILE))
+        load_words(wv[0], wv_words, 0)
+        load_words(wq[1], wq_words, 1)
+        load_scales(sv_rest, wv_scales, slice(N_TILE, N))
+        load_words(wv[1], wv_words, 1)
+        load_x(2)
+        load_words(wq[2], wq_words, 2)
+        load_words(wv[2], wv_words, 2)
+        load_x(3)
+
+        gain_words = gain_rows[:].bitcast(F32)
+        for js in ((0, 1), (2,)):
+            bank = next_bank("tr", TR_BANKS, [P, 4, P])
+            for c, j in enumerate(js):
+                for u in range(2):
+                    nc.tensor.transpose(bank[:, 2 * c + u, :], gain_words[:, j, u : u + 1].to_broadcast([P, P]), ident[:])
+            cols = slice(js[0] * N_TILE, (js[-1] + 1) * N_TILE)
+            nc.vector.tensor_copy(
+                out=gain[:, cols].bitcast(F32).rearrange("p (c q u) -> p c q u", c=len(js), u=2),
+                in_=bank[:, : 2 * len(js), :].rearrange("p (c u) q -> p c q u", u=2),
+            )
+
+        turn_x(0)
+        turn_x(1)
+        early = [project(chunks[i][0], chunks[i][1], True) for i in range(2)]
+        for i in range(2):
+            gain_mul(i, early[i])
+
+        pending = None
+        for i in range(len(chunks)):
+            m, n = chunks[i]
+            if i >= 2:
+                th = project(m, n, True)
+                if pending is not None:
+                    yt = drain_y(*pending)
+                gain_mul(i, th)
+            if i >= 1:
+                cast(i - 1)
+            if pending is not None:
+                quantize_y(pending[0], yt)
+                done = chunks[pending[0][0]][0]
+                if done == groups[0][1] - 1:
+                    store_codes(0, slice(0, N_TILES))
+                if done == groups[1][1] - 1:
+                    store_codes(1, slice(0, N_TILES))
+                    store_scales(y_scales_main, slice(0, 7 * P), [nc.sync] * 4)
+                pending = None
+            th = project(m, n, False)
+            if i < last:
+                product(i, th)
+            if i >= 3 and i % 3 == 0:
+                nxt = i // 3 + 1
+                if nxt + 2 < M_TILES:
+                    load_x(nxt + 2)
+                if nxt < M_TILES:
+                    turn_x(nxt)
+                ids = [i - 3, i - 2]
+                bank = turn_y(ids)
+                quantize_y(ids, drain_y(ids, bank))
+                pending = ([i - 1], turn_y([i - 1]))
+
+        h = work.tile([P, N_TILE], BF16, name="y16", bufs=6, align_bytes=64)
+        nc.vector.tensor_tensor(
+            out=h[:].rearrange("p (u q e) -> p u q e", u=2, e=2),
+            in0=split_view(gained[last][:]),
+            in1=split_view(th[:]),
+            op=MULT,
+        )
+        y16[last] = h
+        product(last, th)
+        ids = [last - 2, last - 1]
+        quantize_y(ids, drain_y(ids, turn_y(ids)))
+        store_codes(2, slice(0, 2))
+        quantize_y([last], drain_y([last], turn_y([last])))
+        store_codes(2, slice(2, 3))
+        store_scales(y_scales_last, slice(7 * P, M), [nc.scalar, nc.sync, nc.scalar, nc.sync])

@@ -54,65 +54,59 @@ def tile_question_image_joint_features_g4_kernel(
         xv = [keep.tile([P, KV], BF16, name="xv%d" % m, align_bytes=64) for m in range(M_TILES)]
         wq = [keep.tile([P, GQ, 2 * N_TILE], U8, name="wq%d" % n, align_bytes=64) for n in range(N_TILES)]
         wv = [keep.tile([P, GV, 2 * N_TILE], U8, name="wv%d" % n, align_bytes=64) for n in range(N_TILES)]
-        sq = keep.tile([P, GQ, N], U8, name="sq", align_bytes=64)
-        sv_first = keep.tile([P, GV, N_TILE], U8, name="sv_first", align_bytes=64)
-        sv_rest = keep.tile([P, GV, N - N_TILE], U8, name="sv_rest", align_bytes=64)
+        sq = [keep.tile([P, GQ, N_TILE], U8, name="sq%d" % n, align_bytes=64) for n in range(N_TILES)]
+        sv = [keep.tile([P, GV, N_TILE], U8, name="sv%d" % n, align_bytes=64) for n in range(N_TILES)]
         groups = [(0, 4), (4, 7), (7, 8)]
         y_codes = [keep.tile([P, N_TILES, (b - a) * P], U32, name="y_codes%d" % a, align_bytes=64) for a, b in groups]
-        y_scales_main = keep.tile([P, N_TILES, 7 * P], U8, name="y_scales_main", align_bytes=64)
-        y_scales_last = keep.tile([P, N_TILES, P], U8, name="y_scales_last", align_bytes=64)
+        y_scales = [keep.tile([P, N_TILES, (b - a) * P], U8, name="y_scales%d" % a, align_bytes=64) for a, b in groups]
+
+        def load_q(m):
+            nc.sync.dma_start(out=xq[m][:], in_=question[m * P : (m + 1) * P, :])
+
+        def load_v(m):
+            nc.sync.dma_start(out=xv[m][:], in_=image[m * P : (m + 1) * P, :])
 
         def load_x(m):
-            rows = slice(m * P, (m + 1) * P)
-            nc.sync.dma_start(out=xq[m][:], in_=question[rows, :])
-            nc.sync.dma_start(out=xv[m][:], in_=image[rows, :])
+            load_q(m)
+            load_v(m)
 
         def load_words(tile, words, n):
             src = words[:, :, 2 * N_TILE * n : 2 * N_TILE * (n + 1)].rearrange("g p b -> p g b")
             nc.sync.dma_start(out=tile[:].bitcast(I32), in_=src.bitcast(I32))
 
-        def load_scales(tile, scales, cols):
-            for q in range(4):
-                src = scales[:, 4 * q : 4 * q + 4, cols].rearrange("g r n -> r g n")
-                nc.sync.dma_start(out=tile[32 * q : 32 * q + 4].bitcast(I32), in_=src.bitcast(I32))
+        def load_scales(tile, scales, n):
+            cols = slice(n * N_TILE, (n + 1) * N_TILE)
+            for r in range(4):
+                src = scales[:, r:16:4, cols].rearrange("g q n -> q g n")
+                nc.sync.dma_start(out=tile[r:P:32].bitcast(I32), in_=src.bitcast(I32))
 
         x_codes = {}
         x_scales = {}
 
-        def turn_x(m):
-            codes = work.tile([P, G * P], U32, name="x_codes", align_bytes=64)
-            scales = work.tile([P, G * P], U8, name="x_scales", align_bytes=64)
-            x_codes[m] = codes
-            x_scales[m] = scales
-            for pair in range(G // 2):
-                src = xq[m] if pair == 0 else xv[m]
-                first = 0 if pair == 0 else (pair - 1) * 2
-                words = src[:].bitcast(F32)
-                bank = next_bank("tr", TR_BANKS, [P, 4, P])
-                for gl in range(2):
-                    g = first + gl
-                    for u in range(2):
-                        nc.tensor.transpose(bank[:, 2 * gl + u, :], words[:, 256 * g + u : 256 * (g + 1) : 2], ident[:])
-                xt = work.tile([P, 2 * K_PASS], BF16, name="xt", align_bytes=64)
-                nc.scalar.copy(
-                    out=xt[:].bitcast(F32).rearrange("p (g m u) -> p g m u", g=2, u=2),
-                    in_=bank[:].rearrange("p (g u) m -> p g m u", u=2),
-                )
-                cols = slice(2 * P * pair, 2 * P * (pair + 1))
-                nc.vector.quantize_mx(out=codes[:, cols].bitcast(FP8X4), scales=scales[:, cols], in_=xt[:])
+        def turn_pair(m, pair):
+            if pair == 0:
+                x_codes[m] = work.tile([P, G * P], U32, name="x_codes", align_bytes=64)
+                x_scales[m] = work.tile([P, G * P], U8, name="x_scales", align_bytes=64)
+            bank = next_bank("tr", TR_BANKS, [P, 4, P])
+            for j in range(4):
+                g = j // 2 if pair == 0 else 2 * (pair - 1) + j // 2
+                words = (xq[m] if pair == 0 else xv[m])[:].bitcast(F32)
+                src = words[:, 256 * g + j % 2 : 256 * (g + 1) : 2]
+                nc.tensor.transpose(bank[:, j, :], src, ident[:])
+            xt = work.tile([P, 2 * K_PASS], BF16, name="xt", align_bytes=64)
+            nc.scalar.copy(
+                out=xt[:].bitcast(F32).rearrange("p (g m u) -> p g m u", g=2, u=2),
+                in_=bank[:].rearrange("p (g u) m -> p g m u", u=2),
+            )
+            cols = slice(2 * P * pair, 2 * P * (pair + 1))
+            nc.vector.quantize_mx(out=x_codes[m][:, cols].bitcast(FP8X4), scales=x_scales[m][:, cols], in_=xt[:])
 
-        def w_scale(is_q, g, n):
-            if is_q:
-                return sq[:, g, n * N_TILE : (n + 1) * N_TILE]
-            if n == 0:
-                return sv_first[:, g, :]
-            return sv_rest[:, g, (n - 1) * N_TILE : n * N_TILE]
-
-        def project(m, n, is_q):
+        def project(m, n, is_q, parts=1):
             acc = next_bank("acc", ACC_BANKS, [P, N_TILE])
             passes = GQ if is_q else GV
             first = 0 if is_q else GQ
             w = wq[n] if is_q else wv[n]
+            s = sq[n] if is_q else sv[n]
             for g in range(passes):
                 cols = slice((first + g) * P, (first + g + 1) * P)
                 nc.tensor.matmul_mx(
@@ -120,12 +114,15 @@ def tile_question_image_joint_features_g4_kernel(
                     lhsT=x_codes[m][:, cols].bitcast(FP8X4),
                     lhsT_scale=x_scales[m][:, cols],
                     rhs=w[:, g, :].bitcast(FP4X4),
-                    rhs_scale=w_scale(is_q, g, n),
+                    rhs_scale=s[:, g, :],
                     start=(g == 0),
                     stop=(g == passes - 1),
                 )
-            th = work.tile([P, N_TILE], F32, name="tanh_q" if is_q else "tanh_v")
-            nc.scalar.activation(out=th[:], in_=acc[:], func=TANH)
+            th = work.tile([P, N_TILE], F32, name="tanh_q" if is_q else "tanh_v", bufs=4)
+            width = N_TILE // parts
+            for part in range(parts):
+                cols = slice(part * width, (part + 1) * width)
+                nc.scalar.activation(out=th[:, cols], in_=acc[:, cols], func=TANH)
             return th
 
         chunks = [(0, 0), (1, 0), (0, 1), (1, 1), (0, 2), (1, 2)]
@@ -178,13 +175,9 @@ def tile_question_image_joint_features_g4_kernel(
                 m, n = chunks[i]
                 k = [j for j, (a, b) in enumerate(groups) if a <= m < b][0]
                 off = (m - groups[k][0]) * P
-                if m < M_TILES - 1:
-                    scales = y_scales_main[:, n, m * P : (m + 1) * P]
-                else:
-                    scales = y_scales_last[:, n, :]
                 nc.vector.quantize_mx(
                     out=y_codes[k][:, n, off : off + P].bitcast(FP8X4),
-                    scales=scales,
+                    scales=y_scales[k][:, n, off : off + P],
                     in_=yt[:, c * N_TILE : (c + 1) * N_TILE],
                 )
 
@@ -193,31 +186,34 @@ def tile_question_image_joint_features_g4_kernel(
             dst = out_1.rearrange("g p m t -> p g (m t)")[:, ns, 4 * P * a : 4 * P * b]
             nc.sync.dma_start(out=dst.bitcast(I32), in_=y_codes[k][:, ns, :].bitcast(I32))
 
-        def store_scales(tile, cols, queues):
-            for q in range(4):
-                dst = out_2[:, 4 * q : 4 * q + 4, cols].rearrange("g r m -> r g m")
-                queues[q].dma_start(out=dst.bitcast(I32), in_=tile[32 * q : 32 * q + 4].bitcast(I32))
+        def store_scales(k, queues):
+            a, b = groups[k]
+            for r in range(4):
+                dst = out_2[:, r:16:4, a * P : b * P].rearrange("g q m -> q g m")
+                queues[r].dma_start(out=dst.bitcast(I32), in_=y_scales[k][r:P:32].bitcast(I32))
 
+        load_q(0)
+        load_q(1)
         nc.sync.dma_start(out=gain_rows[:], in_=joint_gain.rearrange("(j p e) -> p j e", p=P, e=4))
-        load_x(0)
-        load_x(1)
         nc.vector.memset(warm_in[:], 0.0)
         nc.scalar.activation(out=warm_out[:], in_=warm_in[:], func=TANH)
         make_identity(nc, ident[:])
-        for tile in (sq, sv_first, sv_rest):
-            nc.vector.memset(tile[:].rearrange("p g n -> p (g n)").bitcast(I32), 0)
-        load_scales(sq, wq_scales, slice(0, N))
-        load_words(wq[0], wq_words, 0)
-        load_scales(sv_first, wv_scales, slice(0, N_TILE))
-        load_words(wv[0], wv_words, 0)
-        load_words(wq[1], wq_words, 1)
-        load_scales(sv_rest, wv_scales, slice(N_TILE, N))
-        load_words(wv[1], wv_words, 1)
-        load_x(2)
-        load_words(wq[2], wq_words, 2)
-        load_words(wv[2], wv_words, 2)
-        load_x(3)
+        for n in range(N_TILES):
+            for plane in (sq[n], sv[n]):
+                nc.vector.memset(plane[:].rearrange("p g n -> p (g n)").bitcast(I32), 0)
+        for n in range(N_TILES):
+            load_scales(sq[n], wq_scales, n)
+            load_words(wq[n], wq_words, n)
+            if n == 0:
+                load_v(0)
+                load_v(1)
+            load_scales(sv[n], wv_scales, n)
+            load_words(wv[n], wv_words, n)
+            if n >= 1:
+                load_x(n + 1)
 
+        turn_pair(0, 0)
+        turn_pair(1, 0)
         gain_words = gain_rows[:].bitcast(F32)
         for js in ((0, 1), (2,)):
             bank = next_bank("tr", TR_BANKS, [P, 4, P])
@@ -230,9 +226,10 @@ def tile_question_image_joint_features_g4_kernel(
                 in_=bank[:, : 2 * len(js), :].rearrange("p (c u) q -> p c q u", u=2),
             )
 
-        turn_x(0)
-        turn_x(1)
         early = [project(chunks[i][0], chunks[i][1], True) for i in range(2)]
+        for m in range(2):
+            turn_pair(m, 1)
+            turn_pair(m, 2)
         for i in range(2):
             gain_mul(i, early[i])
 
@@ -244,18 +241,17 @@ def tile_question_image_joint_features_g4_kernel(
                 if pending is not None:
                     yt = drain_y(*pending)
                 gain_mul(i, th)
-            if i >= 1:
+            if i >= 1 and (i - 1) not in y16:
                 cast(i - 1)
             if pending is not None:
                 quantize_y(pending[0], yt)
                 done = chunks[pending[0][0]][0]
-                if done == groups[0][1] - 1:
-                    store_codes(0, slice(0, N_TILES))
-                if done == groups[1][1] - 1:
-                    store_codes(1, slice(0, N_TILES))
-                    store_scales(y_scales_main, slice(0, 7 * P), [nc.sync] * 4)
+                for k in range(2):
+                    if done == groups[k][1] - 1:
+                        store_codes(k, slice(0, N_TILES))
+                        store_scales(k, [nc.sync] * 4)
                 pending = None
-            th = project(m, n, False)
+            th = project(m, n, False, 2 if i == last else 1)
             if i < last:
                 product(i, th)
             if i >= 3 and i % 3 == 0:
@@ -263,19 +259,24 @@ def tile_question_image_joint_features_g4_kernel(
                 if nxt + 2 < M_TILES:
                     load_x(nxt + 2)
                 if nxt < M_TILES:
-                    turn_x(nxt)
+                    turn_pair(nxt, 0)
+                    cast(i)
+                    turn_pair(nxt, 1)
+                    turn_pair(nxt, 2)
                 ids = [i - 3, i - 2]
                 bank = turn_y(ids)
                 quantize_y(ids, drain_y(ids, bank))
                 pending = ([i - 1], turn_y([i - 1]))
 
         h = work.tile([P, N_TILE], BF16, name="y16", bufs=6, align_bytes=64)
-        nc.vector.tensor_tensor(
-            out=h[:].rearrange("p (u q e) -> p u q e", u=2, e=2),
-            in0=split_view(gained[last][:]),
-            in1=split_view(th[:]),
-            op=MULT,
-        )
+        for part in range(2):
+            cols = slice(part * N_TILE // 2, (part + 1) * N_TILE // 2)
+            nc.vector.tensor_tensor(
+                out=h[:].rearrange("p (u q e) -> p u q e", u=2, e=2)[:, :, part * P // 2 : (part + 1) * P // 2, :],
+                in0=split_view(gained[last][:, cols]),
+                in1=split_view(th[:, cols]),
+                op=MULT,
+            )
         y16[last] = h
         product(last, th)
         ids = [last - 2, last - 1]
@@ -283,4 +284,4 @@ def tile_question_image_joint_features_g4_kernel(
         store_codes(2, slice(0, 2))
         quantize_y([last], drain_y([last], turn_y([last])))
         store_codes(2, slice(2, 3))
-        store_scales(y_scales_last, slice(7 * P, M), [nc.scalar, nc.sync, nc.scalar, nc.sync])
+        store_scales(2, [nc.scalar, nc.sync, nc.scalar, nc.sync])

@@ -17,15 +17,16 @@ TANH = mybir.ActivationFunctionType.Tanh
 MULT = mybir.AluOpType.mult
 
 P = 128
-K_PASS = 512
-N_TILE = 512
-GQ = KQ // K_PASS
-GV = KV // K_PASS
-G = GQ + GV
-M_TILES = M // P
-N_TILES = N // N_TILE
+GROUP = 512
+WORDS = GROUP // 2
+GQ, GV = KQ // GROUP, KV // GROUP
+M_TILES, N_TILES = M // P, N // GROUP
 ACC_BANKS = 4
-TR_BANKS = 4
+TURN_BANKS = 4
+QUESTION, IMAGE_LO, IMAGE_HI = 0, 1, 2
+STORE_RANGES = [(0, 4), (4, 7), (7, 8)]
+CHUNKS = [(m, n) for n in range(N_TILES) for m in range(2)]
+CHUNKS = CHUNKS + [(m, n) for m in range(2, M_TILES) for n in range(N_TILES)]
 
 
 def tile_question_image_joint_features_g4_kernel(
@@ -38,11 +39,11 @@ def tile_question_image_joint_features_g4_kernel(
         psum = ctx.enter_context(tc.psum_pool(name="psum", bufs=1))
         ctx.enter_context(tc.manual_schedule())
 
-        counters = {"acc": 0, "tr": 0}
+        banks_taken = {"acc": 0, "turn": 0}
 
-        def next_bank(kind, banks, shape):
-            name = "%s%d" % (kind, counters[kind] % banks)
-            counters[kind] = counters[kind] + 1
+        def next_bank(kind, count, shape):
+            name = "%s%d" % (kind, banks_taken[kind] % count)
+            banks_taken[kind] = banks_taken[kind] + 1
             return psum.tile(shape, F32, name=name, tag=name)
 
         ident = keep.tile([P, P], F32, name="ident", align_bytes=64)
@@ -52,109 +53,144 @@ def tile_question_image_joint_features_g4_kernel(
         gain = keep.tile([P, N], BF16, name="gain", align_bytes=64)
         xq = [keep.tile([P, KQ], BF16, name="xq%d" % m, align_bytes=64) for m in range(M_TILES)]
         xv = [keep.tile([P, KV], BF16, name="xv%d" % m, align_bytes=64) for m in range(M_TILES)]
-        wq = [keep.tile([P, GQ, 2 * N_TILE], U8, name="wq%d" % n, align_bytes=64) for n in range(N_TILES)]
-        wv = [keep.tile([P, GV, 2 * N_TILE], U8, name="wv%d" % n, align_bytes=64) for n in range(N_TILES)]
-        sq = [keep.tile([P, GQ, N_TILE], U8, name="sq%d" % n, align_bytes=64) for n in range(N_TILES)]
-        sv = [keep.tile([P, GV, N_TILE], U8, name="sv%d" % n, align_bytes=64) for n in range(N_TILES)]
-        groups = [(0, 4), (4, 7), (7, 8)]
-        y_codes = [keep.tile([P, N_TILES, (b - a) * P], U32, name="y_codes%d" % a, align_bytes=64) for a, b in groups]
-        y_scales = [keep.tile([P, N_TILES, (b - a) * P], U8, name="y_scales%d" % a, align_bytes=64) for a, b in groups]
+        wq = [keep.tile([P, GQ, 2 * GROUP], U8, name="wq%d" % n, align_bytes=64) for n in range(N_TILES)]
+        wv = [keep.tile([P, GV, 2 * GROUP], U8, name="wv%d" % n, align_bytes=64) for n in range(N_TILES)]
+        sq = [keep.tile([P, GQ, GROUP], U8, name="sq%d" % n, align_bytes=64) for n in range(N_TILES)]
+        sv = [keep.tile([P, GV, GROUP], U8, name="sv%d" % n, align_bytes=64) for n in range(N_TILES)]
+        y_codes = [keep.tile([P, N_TILES, (b - a) * P], U32, name="y_codes%d" % a, align_bytes=64) for a, b in STORE_RANGES]
+        y_scales = [keep.tile([P, N_TILES, (b - a) * P], U8, name="y_scales%d" % a, align_bytes=64) for a, b in STORE_RANGES]
 
-        def load_q(m):
+        def columns(n):
+            return slice(n * GROUP, (n + 1) * GROUP)
+
+
+        def load_question(m):
             nc.sync.dma_start(out=xq[m][:], in_=question[m * P : (m + 1) * P, :])
 
-        def load_v(m):
+        def load_image(m):
             nc.sync.dma_start(out=xv[m][:], in_=image[m * P : (m + 1) * P, :])
 
-        def load_x(m):
-            load_q(m)
-            load_v(m)
+        def load_rows(m):
+            load_question(m)
+            load_image(m)
 
-        def load_words(tile, words, n):
-            src = words[:, :, 2 * N_TILE * n : 2 * N_TILE * (n + 1)].rearrange("g p b -> p g b")
-            nc.sync.dma_start(out=tile[:].bitcast(I32), in_=src.bitcast(I32))
-
-        def load_scales(tile, scales, n):
-            cols = slice(n * N_TILE, (n + 1) * N_TILE)
+        def load_weights(codes, plane, words, scales, n):
             for r in range(4):
-                src = scales[:, r:16:4, cols].rearrange("g q n -> q g n")
-                nc.sync.dma_start(out=tile[r:P:32].bitcast(I32), in_=src.bitcast(I32))
+                rows = scales[:, r:16:4, columns(n)].rearrange("g q n -> q g n")
+                nc.sync.dma_start(out=plane[r:P:32].bitcast(I32), in_=rows.bitcast(I32))
+            src = words[:, :, 2 * GROUP * n : 2 * GROUP * (n + 1)].rearrange("g p b -> p g b")
+            nc.sync.dma_start(out=codes[:].bitcast(I32), in_=src.bitcast(I32))
 
-        x_codes = {}
-        x_scales = {}
+        def store_codes(k, groups):
+            a, b = STORE_RANGES[k]
+            dst = out_1.rearrange("g p m t -> p g (m t)")[:, groups, 4 * P * a : 4 * P * b]
+            nc.sync.dma_start(out=dst.bitcast(I32), in_=y_codes[k][:, groups, :].bitcast(I32))
 
-        def turn_pair(m, pair):
-            if pair == 0:
-                x_codes[m] = work.tile([P, G * P], U32, name="x_codes", align_bytes=64)
-                x_scales[m] = work.tile([P, G * P], U8, name="x_scales", align_bytes=64)
-            bank = next_bank("tr", TR_BANKS, [P, 4, P])
-            for j in range(4):
-                g = j // 2 if pair == 0 else 2 * (pair - 1) + j // 2
-                words = (xq[m] if pair == 0 else xv[m])[:].bitcast(F32)
-                src = words[:, 256 * g + j % 2 : 256 * (g + 1) : 2]
-                nc.tensor.transpose(bank[:, j, :], src, ident[:])
-            xt = work.tile([P, 2 * K_PASS], BF16, name="xt", align_bytes=64)
-            nc.scalar.copy(
-                out=xt[:].bitcast(F32).rearrange("p (g m u) -> p g m u", g=2, u=2),
-                in_=bank[:].rearrange("p (g u) m -> p g m u", u=2),
+        def store_scales(k, queues):
+            a, b = STORE_RANGES[k]
+            for r in range(4):
+                dst = out_2[:, r:16:4, a * P : b * P].rearrange("g q m -> q g m")
+                queues[r].dma_start(out=dst.bitcast(I32), in_=y_scales[k][r:P:32].bitcast(I32))
+
+
+        x_codes, x_scales, sorted_words = {}, {}, {}
+
+        def part_words(m, part):
+            if part == QUESTION:
+                return xq[m][:].bitcast(F32)
+            return xv[m][:].bitcast(F32)[:, columns(part - IMAGE_LO)]
+
+        def sort_words(m, part, copy):
+            dst = work.tile([P, 2 * WORDS], F32, name="sorted%d" % part, align_bytes=64)
+            copy(
+                out=dst[:].rearrange("p (g u q) -> p g q u", g=2, u=2),
+                in_=part_words(m, part).rearrange("p (g q u) -> p g q u", g=2, u=2),
             )
-            cols = slice(2 * P * pair, 2 * P * (pair + 1))
-            nc.vector.quantize_mx(out=x_codes[m][:, cols].bitcast(FP8X4), scales=x_scales[m][:, cols], in_=xt[:])
+            sorted_words[m, part] = dst
 
-        def project(m, n, is_q, parts=1):
-            acc = next_bank("acc", ACC_BANKS, [P, N_TILE])
-            passes = GQ if is_q else GV
-            first = 0 if is_q else GQ
-            w = wq[n] if is_q else wv[n]
-            s = sq[n] if is_q else sv[n]
+        def copy_out(dst, bank, groups, copy):
+            copy(
+                out=dst.bitcast(F32).rearrange("p (g c u) -> p g c u", g=groups, u=2),
+                in_=bank[:, : 2 * groups, :].rearrange("p (g u) c -> p g c u", u=2),
+            )
+
+        def turn_x(m, part):
+            bank = next_bank("turn", TURN_BANKS, [P, 4, P])
+            for g in range(2):
+                for u in range(2):
+                    if (m, part) in sorted_words:
+                        src = sorted_words[m, part][:, (2 * g + u) * P : (2 * g + u + 1) * P]
+                    else:
+                        src = part_words(m, part)[:, WORDS * g + u : WORDS * (g + 1) : 2]
+                    nc.tensor.transpose(bank[:, 2 * g + u, :], src, ident[:])
+            turned = work.tile([P, 2 * GROUP], BF16, name="x_turned", align_bytes=64)
+            copy_out(turned[:], bank, 2, nc.scalar.copy)
+            return turned
+
+        def quantize_x(m, part, turned):
+            if part == QUESTION:
+                x_codes[m] = work.tile([P, (GQ + GV) * P], U32, name="x_codes", align_bytes=64)
+                x_scales[m] = work.tile([P, (GQ + GV) * P], U8, name="x_scales", align_bytes=64)
+            cols = slice(2 * P * part, 2 * P * (part + 1))
+            nc.vector.quantize_mx(out=x_codes[m][:, cols].bitcast(FP8X4), scales=x_scales[m][:, cols], in_=turned[:])
+
+        def prepare_x(m, part):
+            quantize_x(m, part, turn_x(m, part))
+
+
+        tanh_q, tanh_v, gained, y32, y16 = {}, {}, {}, {}, {}
+
+        def project(i, codes, plane, first, passes, name, parts):
+            m = CHUNKS[i][0]
+            acc = next_bank("acc", ACC_BANKS, [P, GROUP])
             for g in range(passes):
                 cols = slice((first + g) * P, (first + g + 1) * P)
                 nc.tensor.matmul_mx(
                     out=acc[:],
                     lhsT=x_codes[m][:, cols].bitcast(FP8X4),
                     lhsT_scale=x_scales[m][:, cols],
-                    rhs=w[:, g, :].bitcast(FP4X4),
-                    rhs_scale=s[:, g, :],
+                    rhs=codes[:, g, :].bitcast(FP4X4),
+                    rhs_scale=plane[:, g, :],
                     start=(g == 0),
                     stop=(g == passes - 1),
                 )
-            th = work.tile([P, N_TILE], F32, name="tanh_q" if is_q else "tanh_v", bufs=4)
-            width = N_TILE // parts
-            for part in range(parts):
-                cols = slice(part * width, (part + 1) * width)
-                nc.scalar.activation(out=th[:, cols], in_=acc[:, cols], func=TANH)
-            return th
+            result = work.tile([P, GROUP], F32, name=name, bufs=4)
+            for j in range(parts):
+                cols = slice(j * GROUP // parts, (j + 1) * GROUP // parts)
+                nc.scalar.activation(out=result[:, cols], in_=acc[:, cols], func=TANH)
+            return result
 
-        chunks = [(0, 0), (1, 0), (0, 1), (1, 1), (0, 2), (1, 2)]
-        chunks = chunks + [(m, n) for m in range(2, M_TILES) for n in range(N_TILES)]
-        last = len(chunks) - 1
-        gained = {}
-        y32 = {}
-        y16 = {}
+        def question_side(i):
+            n = CHUNKS[i][1]
+            tanh_q[i] = project(i, wq[n], sq[n], 0, GQ, "tanh_q", 1)
 
-        def gain_mul(i, th):
-            n = chunks[i][1]
-            t = work.tile([P, N_TILE], F32, name="gained")
-            nc.vector.tensor_tensor(out=t[:], in0=th[:], in1=gain[:, n * N_TILE : (n + 1) * N_TILE], op=MULT)
-            gained[i] = t
+        def image_side(i, parts=1):
+            n = CHUNKS[i][1]
+            tanh_v[i] = project(i, wv[n], sv[n], GQ, GV, "tanh_v", parts)
 
-        def product(i, th):
-            m, n = chunks[i]
-            y = work.tile([P, N_TILE], F32, name="y32", bufs=5)
-            nc.vector.tensor_tensor(out=y[:], in0=gained[i][:], in1=th[:], op=MULT)
-            y32[i] = y
-            nc.sync.dma_start(out=out_0[m * P : (m + 1) * P, n * N_TILE : (n + 1) * N_TILE], in_=y[:])
+        def apply_gain(i):
+            gained[i] = work.tile([P, GROUP], F32, name="gained", bufs=4)
+            nc.vector.tensor_tensor(out=gained[i][:], in0=tanh_q[i][:], in1=gain[:, columns(CHUNKS[i][1])], op=MULT)
 
-        def split_view(ap):
+        def product(i):
+            m, n = CHUNKS[i]
+            y32[i] = work.tile([P, GROUP], F32, name="y32", bufs=8)
+            nc.vector.tensor_tensor(out=y32[i][:], in0=gained[i][:], in1=tanh_v[i][:], op=MULT)
+            nc.sync.dma_start(out=out_0[m * P : (m + 1) * P, columns(n)], in_=y32[i][:])
+
+
+        def by_word_parity(ap):
             return ap.rearrange("p (q u e) -> p u q e", u=2, e=2)
 
-        def cast(i):
-            h = work.tile([P, N_TILE], BF16, name="y16", bufs=6, align_bytes=64)
-            nc.vector.tensor_copy(out=h[:].rearrange("p (u q e) -> p u q e", u=2, e=2), in_=split_view(y32[i][:]))
-            y16[i] = h
+        def new_y16(i):
+            y16[i] = work.tile([P, GROUP], BF16, name="y16", bufs=6, align_bytes=64)
+            return y16[i][:].rearrange("p (u q e) -> p u q e", u=2, e=2)
+
+        def round_y(i, copy):
+            copy(out=new_y16(i), in_=by_word_parity(y32[i][:]))
 
         def turn_y(ids):
-            bank = next_bank("tr", TR_BANKS, [P, 4, P])
+            bank = next_bank("turn", TURN_BANKS, [P, 4, P])
             for c, i in enumerate(ids):
                 words = y16[i][:].bitcast(F32)
                 for u in range(2):
@@ -162,38 +198,28 @@ def tile_question_image_joint_features_g4_kernel(
             return bank
 
         def drain_y(ids, bank):
-            count = len(ids)
-            yt = work.tile([P, 2 * N_TILE], BF16, name="yt", align_bytes=64)
-            nc.scalar.copy(
-                out=yt[:, : count * N_TILE].bitcast(F32).rearrange("p (c m u) -> p c m u", c=count, u=2),
-                in_=bank[:, : 2 * count, :].rearrange("p (c u) m -> p c m u", u=2),
-            )
-            return yt
+            turned = work.tile([P, 2 * GROUP], BF16, name="y_turned", bufs=4, align_bytes=64)
+            copy_out(turned[:, : len(ids) * GROUP], bank, len(ids), nc.scalar.copy)
+            return turned
 
-        def quantize_y(ids, yt):
+        chunks_left = [(b - a) * N_TILES for a, b in STORE_RANGES]
+
+        def quantize_y(ids, turned):
             for c, i in enumerate(ids):
-                m, n = chunks[i]
-                k = [j for j, (a, b) in enumerate(groups) if a <= m < b][0]
-                off = (m - groups[k][0]) * P
+                m, n = CHUNKS[i]
+                k = [j for j, (a, b) in enumerate(STORE_RANGES) if a <= m < b][0]
+                cols = slice((m - STORE_RANGES[k][0]) * P, (m - STORE_RANGES[k][0] + 1) * P)
                 nc.vector.quantize_mx(
-                    out=y_codes[k][:, n, off : off + P].bitcast(FP8X4),
-                    scales=y_scales[k][:, n, off : off + P],
-                    in_=yt[:, c * N_TILE : (c + 1) * N_TILE],
+                    out=y_codes[k][:, n, cols].bitcast(FP8X4), scales=y_scales[k][:, n, cols], in_=turned[:, columns(c)]
                 )
+                chunks_left[k] = chunks_left[k] - 1
+                if chunks_left[k] == 0 and k < len(STORE_RANGES) - 1:
+                    store_codes(k, slice(0, N_TILES))
+                    store_scales(k, [nc.sync] * 4)
 
-        def store_codes(k, ns):
-            a, b = groups[k]
-            dst = out_1.rearrange("g p m t -> p g (m t)")[:, ns, 4 * P * a : 4 * P * b]
-            nc.sync.dma_start(out=dst.bitcast(I32), in_=y_codes[k][:, ns, :].bitcast(I32))
 
-        def store_scales(k, queues):
-            a, b = groups[k]
-            for r in range(4):
-                dst = out_2[:, r:16:4, a * P : b * P].rearrange("g q m -> q g m")
-                queues[r].dma_start(out=dst.bitcast(I32), in_=y_scales[k][r:P:32].bitcast(I32))
-
-        load_q(0)
-        load_q(1)
+        load_question(0)
+        load_question(1)
         nc.sync.dma_start(out=gain_rows[:], in_=joint_gain.rearrange("(j p e) -> p j e", p=P, e=4))
         nc.vector.memset(warm_in[:], 0.0)
         nc.scalar.activation(out=warm_out[:], in_=warm_in[:], func=TANH)
@@ -202,86 +228,124 @@ def tile_question_image_joint_features_g4_kernel(
             for plane in (sq[n], sv[n]):
                 nc.vector.memset(plane[:].rearrange("p g n -> p (g n)").bitcast(I32), 0)
         for n in range(N_TILES):
-            load_scales(sq[n], wq_scales, n)
-            load_words(wq[n], wq_words, n)
+            load_weights(wq[n], sq[n], wq_words, wq_scales, n)
             if n == 0:
-                load_v(0)
-                load_v(1)
-            load_scales(sv[n], wv_scales, n)
-            load_words(wv[n], wv_words, n)
-            if n >= 1:
-                load_x(n + 1)
+                load_image(0)
+                load_image(1)
+            load_weights(wv[n], sv[n], wv_words, wv_scales, n)
+            if n > 0:
+                load_rows(n + 1)
+        load_rows(4)
 
-        turn_pair(0, 0)
-        turn_pair(1, 0)
+        prepare_x(0, QUESTION)
+        prepare_x(1, QUESTION)
         gain_words = gain_rows[:].bitcast(F32)
-        for js in ((0, 1), (2,)):
-            bank = next_bank("tr", TR_BANKS, [P, 4, P])
-            for c, j in enumerate(js):
+        for tiles in ([0, 1], [2]):
+            bank = next_bank("turn", TURN_BANKS, [P, 4, P])
+            for c, n in enumerate(tiles):
                 for u in range(2):
-                    nc.tensor.transpose(bank[:, 2 * c + u, :], gain_words[:, j, u : u + 1].to_broadcast([P, P]), ident[:])
-            cols = slice(js[0] * N_TILE, (js[-1] + 1) * N_TILE)
-            nc.vector.tensor_copy(
-                out=gain[:, cols].bitcast(F32).rearrange("p (c q u) -> p c q u", c=len(js), u=2),
-                in_=bank[:, : 2 * len(js), :].rearrange("p (c u) q -> p c q u", u=2),
-            )
+                    nc.tensor.transpose(bank[:, 2 * c + u, :], gain_words[:, n, u : u + 1].to_broadcast([P, P]), ident[:])
+            copy_out(gain[:, tiles[0] * GROUP : (tiles[-1] + 1) * GROUP], bank, len(tiles), nc.vector.tensor_copy)
 
-        early = [project(chunks[i][0], chunks[i][1], True) for i in range(2)]
-        for m in range(2):
-            turn_pair(m, 1)
-            turn_pair(m, 2)
-        for i in range(2):
-            gain_mul(i, early[i])
+        question_side(0)
+        prepare_x(0, IMAGE_LO)
+        prepare_x(0, IMAGE_HI)
+        apply_gain(0)
+        prepare_x(1, IMAGE_LO)
+        prepare_x(1, IMAGE_HI)
+        question_side(1)
+        image_side(0)
+        apply_gain(1)
+        product(0)
+        image_side(1)
+        round_y(0, nc.vector.tensor_copy)
+        product(1)
+        question_side(2)
+        apply_gain(2)
+        round_y(1, nc.vector.tensor_copy)
+        image_side(2)
+        product(2)
 
-        pending = None
-        for i in range(len(chunks)):
-            m, n = chunks[i]
-            if i >= 2:
-                th = project(m, n, True)
-                if pending is not None:
-                    yt = drain_y(*pending)
-                gain_mul(i, th)
-            if i >= 1 and (i - 1) not in y16:
-                cast(i - 1)
-            if pending is not None:
-                quantize_y(pending[0], yt)
-                done = chunks[pending[0][0]][0]
-                for k in range(2):
-                    if done == groups[k][1] - 1:
-                        store_codes(k, slice(0, N_TILES))
-                        store_scales(k, [nc.sync] * 4)
-                pending = None
-            th = project(m, n, False, 2 if i == last else 1)
-            if i < last:
-                product(i, th)
-            if i >= 3 and i % 3 == 0:
-                nxt = i // 3 + 1
-                if nxt + 2 < M_TILES:
-                    load_x(nxt + 2)
-                if nxt < M_TILES:
-                    turn_pair(nxt, 0)
-                    cast(i)
-                    turn_pair(nxt, 1)
-                    turn_pair(nxt, 2)
-                ids = [i - 3, i - 2]
-                bank = turn_y(ids)
-                quantize_y(ids, drain_y(ids, bank))
-                pending = ([i - 1], turn_y([i - 1]))
 
-        h = work.tile([P, N_TILE], BF16, name="y16", bufs=6, align_bytes=64)
-        for part in range(2):
-            cols = slice(part * N_TILE // 2, (part + 1) * N_TILE // 2)
+        for i in range(N_TILES, len(CHUNKS) - N_TILES, N_TILES):
+            turning = i // N_TILES + 1
+            question_side(i)
+            apply_gain(i)
+            round_y(i - 1, nc.vector.tensor_copy)
+            image_side(i)
+            if turning + 3 < M_TILES:
+                load_rows(turning + 3)
+            turned_question = turn_x(turning, QUESTION)
+            if 3 < turning + 1 < M_TILES:
+                sort_words(turning + 1, IMAGE_LO, nc.vector.tensor_copy)
+            pair, single = [i - 3, i - 2], [i - 1]
+            turned_pair = drain_y(pair, turn_y(pair))
+            product(i)
+            quantize_x(turning, QUESTION, turned_question)
+            turned_lo = turn_x(turning, IMAGE_LO)
+            turned_hi = turn_x(turning, IMAGE_HI)
+            bank = turn_y(single)
+            quantize_x(turning, IMAGE_LO, turned_lo)
+            quantize_y(pair, turned_pair)
+
+            question_side(i + 1)
+            turned_single = drain_y(single, bank)
+            round_y(i, nc.vector.tensor_copy)
+            apply_gain(i + 1)
+            image_side(i + 1)
+            quantize_x(turning, IMAGE_HI, turned_hi)
+            product(i + 1)
+
+            question_side(i + 2)
+            if turning + 1 < M_TILES:
+                sort_words(turning + 1, QUESTION, nc.scalar.copy)
+            apply_gain(i + 2)
+            round_y(i + 1, nc.vector.tensor_copy)
+            image_side(i + 2)
+            product(i + 2)
+            quantize_y(single, turned_single)
+
+
+        i = len(CHUNKS) - N_TILES
+        question_side(i)
+        question_side(i + 1)
+        round_y(i - 1, nc.vector.tensor_copy)
+        apply_gain(i)
+        apply_gain(i + 1)
+        image_side(i)
+        pair, single = [i - 3, i - 2], [i - 1]
+        pair_bank = turn_y(pair)
+        single_bank = turn_y(single)
+        product(i)
+        turned_pair = drain_y(pair, pair_bank)
+        turned_single = drain_y(single, single_bank)
+        quantize_y(pair, turned_pair)
+        image_side(i + 1)
+        question_side(i + 2)
+        round_y(i, nc.scalar.copy)
+        quantize_y(single, turned_single)
+        product(i + 1)
+        apply_gain(i + 2)
+        image_side(i + 2, 2)
+        round_y(i + 1, nc.vector.tensor_copy)
+        rounded = new_y16(i + 2)
+        for half in range(2):
+            cols = slice(half * GROUP // 2, (half + 1) * GROUP // 2)
             nc.vector.tensor_tensor(
-                out=h[:].rearrange("p (u q e) -> p u q e", u=2, e=2)[:, :, part * P // 2 : (part + 1) * P // 2, :],
-                in0=split_view(gained[last][:, cols]),
-                in1=split_view(th[:, cols]),
+                out=rounded[:, :, half * P // 2 : (half + 1) * P // 2, :],
+                in0=by_word_parity(gained[i + 2][:, cols]),
+                in1=by_word_parity(tanh_v[i + 2][:, cols]),
                 op=MULT,
             )
-        y16[last] = h
-        product(last, th)
-        ids = [last - 2, last - 1]
-        quantize_y(ids, drain_y(ids, turn_y(ids)))
-        store_codes(2, slice(0, 2))
-        quantize_y([last], drain_y([last], turn_y([last])))
-        store_codes(2, slice(2, 3))
-        store_scales(2, [nc.scalar, nc.sync, nc.scalar, nc.sync])
+        product(i + 2)
+        pair, single = [i, i + 1], [i + 2]
+        pair_bank = turn_y(pair)
+        single_bank = turn_y(single)
+        turned_pair = drain_y(pair, pair_bank)
+        turned_single = drain_y(single, single_bank)
+        last_range = len(STORE_RANGES) - 1
+        quantize_y(pair, turned_pair)
+        store_codes(last_range, slice(0, 2))
+        quantize_y(single, turned_single)
+        store_codes(last_range, slice(2, 3))
+        store_scales(last_range, [nc.scalar, nc.sync, nc.scalar, nc.sync])

from contextlib import ExitStack

import concourse.mybir as mybir
from concourse.masks import make_identity

M, KQ, KV, N = 1024, 1024, 2048, 1536
FLOPS = 2 * M * (KQ + KV) * N

F32 = mybir.dt.float32
BF16 = mybir.dt.bfloat16
I32 = mybir.dt.int32
U32 = mybir.dt.uint32
U8 = mybir.dt.uint8
FP8X4 = mybir.dt.float8_e4m3fn_x4
FP4X4 = mybir.dt.float4_e2m1fn_x4
TANH = mybir.ActivationFunctionType.Tanh
MULT = mybir.AluOpType.mult

P = 128
GROUP = 512
WORDS = GROUP // 2
GQ, GV = KQ // GROUP, KV // GROUP
M_TILES, N_TILES = M // P, N // GROUP
ACC_BANKS = 4
TURN_BANKS = 4
QUESTION, IMAGE_LO, IMAGE_HI = 0, 1, 2
STORE_RANGES = [(0, 4), (4, 7), (7, 8)]
CHUNKS = [(m, n) for n in range(N_TILES) for m in range(2)]
CHUNKS = CHUNKS + [(m, n) for m in range(2, M_TILES) for n in range(N_TILES)]


def tile_question_image_joint_features_g4_kernel(
    tc, question, image, wq_words, wq_scales, wv_words, wv_scales, joint_gain, out_0, out_1, out_2
):
    nc = tc.nc
    with ExitStack() as ctx:
        keep = ctx.enter_context(tc.tile_pool(name="keep", bufs=1))
        work = ctx.enter_context(tc.tile_pool(name="work", bufs=3))
        psum = ctx.enter_context(tc.psum_pool(name="psum", bufs=1))
        ctx.enter_context(tc.manual_schedule())

        banks_taken = {"acc": 0, "turn": 0}

        def next_bank(kind, count, shape):
            name = "%s%d" % (kind, banks_taken[kind] % count)
            banks_taken[kind] = banks_taken[kind] + 1
            return psum.tile(shape, F32, name=name, tag=name)

        ident = keep.tile([P, P], F32, name="ident", align_bytes=64)
        warm_in = keep.tile([P, 8], F32, name="warm_in")
        warm_out = keep.tile([P, 8], F32, name="warm_out")
        gain_rows = keep.tile([P, N_TILES, 4], BF16, name="gain_rows")
        gain = keep.tile([P, N], BF16, name="gain", align_bytes=64)
        xq = [keep.tile([P, KQ], BF16, name="xq%d" % m, align_bytes=64) for m in range(M_TILES)]
        xv = [keep.tile([P, KV], BF16, name="xv%d" % m, align_bytes=64) for m in range(M_TILES)]
        wq = [keep.tile([P, GQ, 2 * GROUP], U8, name="wq%d" % n, align_bytes=64) for n in range(N_TILES)]
        wv = [keep.tile([P, GV, 2 * GROUP], U8, name="wv%d" % n, align_bytes=64) for n in range(N_TILES)]
        sq = [keep.tile([P, GQ, GROUP], U8, name="sq%d" % n, align_bytes=64) for n in range(N_TILES)]
        sv = [keep.tile([P, GV, GROUP], U8, name="sv%d" % n, align_bytes=64) for n in range(N_TILES)]
        y_codes = [keep.tile([P, N_TILES, (b - a) * P], U32, name="y_codes%d" % a, align_bytes=64) for a, b in STORE_RANGES]
        y_scales = [keep.tile([P, N_TILES, (b - a) * P], U8, name="y_scales%d" % a, align_bytes=64) for a, b in STORE_RANGES]

        def columns(n):
            return slice(n * GROUP, (n + 1) * GROUP)


        def load_question(m):
            nc.sync.dma_start(out=xq[m][:], in_=question[m * P : (m + 1) * P, :])

        def load_image(m):
            nc.sync.dma_start(out=xv[m][:], in_=image[m * P : (m + 1) * P, :])

        def load_rows(m):
            load_question(m)
            load_image(m)

        def load_weights(codes, plane, words, scales, n):
            for r in range(4):
                rows = scales[:, r:16:4, columns(n)].rearrange("g q n -> q g n")
                nc.sync.dma_start(out=plane[r:P:32].bitcast(I32), in_=rows.bitcast(I32))
            src = words[:, :, 2 * GROUP * n : 2 * GROUP * (n + 1)].rearrange("g p b -> p g b")
            nc.sync.dma_start(out=codes[:].bitcast(I32), in_=src.bitcast(I32))

        def store_codes(k, groups):
            a, b = STORE_RANGES[k]
            dst = out_1.rearrange("g p m t -> p g (m t)")[:, groups, 4 * P * a : 4 * P * b]
            nc.sync.dma_start(out=dst.bitcast(I32), in_=y_codes[k][:, groups, :].bitcast(I32))

        def store_scales(k, queues):
            a, b = STORE_RANGES[k]
            for r in range(4):
                dst = out_2[:, r:16:4, a * P : b * P].rearrange("g q m -> q g m")
                queues[r].dma_start(out=dst.bitcast(I32), in_=y_scales[k][r:P:32].bitcast(I32))


        x_codes, x_scales, sorted_words = {}, {}, {}

        def part_words(m, part):
            if part == QUESTION:
                return xq[m][:].bitcast(F32)
            return xv[m][:].bitcast(F32)[:, columns(part - IMAGE_LO)]

        def sort_words(m, part, copy):
            dst = work.tile([P, 2 * WORDS], F32, name="sorted%d" % part, align_bytes=64)
            copy(
                out=dst[:].rearrange("p (g u q) -> p g q u", g=2, u=2),
                in_=part_words(m, part).rearrange("p (g q u) -> p g q u", g=2, u=2),
            )
            sorted_words[m, part] = dst

        def copy_out(dst, bank, groups, copy):
            copy(
                out=dst.bitcast(F32).rearrange("p (g c u) -> p g c u", g=groups, u=2),
                in_=bank[:, : 2 * groups, :].rearrange("p (g u) c -> p g c u", u=2),
            )

        def turn_x(m, part):
            bank = next_bank("turn", TURN_BANKS, [P, 4, P])
            for g in range(2):
                for u in range(2):
                    if (m, part) in sorted_words:
                        src = sorted_words[m, part][:, (2 * g + u) * P : (2 * g + u + 1) * P]
                    else:
                        src = part_words(m, part)[:, WORDS * g + u : WORDS * (g + 1) : 2]
                    nc.tensor.transpose(bank[:, 2 * g + u, :], src, ident[:])
            turned = work.tile([P, 2 * GROUP], BF16, name="x_turned", align_bytes=64)
            copy_out(turned[:], bank, 2, nc.scalar.copy)
            return turned

        def quantize_x(m, part, turned):
            if part == QUESTION:
                x_codes[m] = work.tile([P, (GQ + GV) * P], U32, name="x_codes", align_bytes=64)
                x_scales[m] = work.tile([P, (GQ + GV) * P], U8, name="x_scales", align_bytes=64)
            cols = slice(2 * P * part, 2 * P * (part + 1))
            nc.vector.quantize_mx(out=x_codes[m][:, cols].bitcast(FP8X4), scales=x_scales[m][:, cols], in_=turned[:])

        def prepare_x(m, part):
            quantize_x(m, part, turn_x(m, part))


        tanh_q, tanh_v, gained, y32, y16 = {}, {}, {}, {}, {}

        def project(i, codes, plane, first, passes, name, parts):
            m = CHUNKS[i][0]
            acc = next_bank("acc", ACC_BANKS, [P, GROUP])
            for g in range(passes):
                cols = slice((first + g) * P, (first + g + 1) * P)
                nc.tensor.matmul_mx(
                    out=acc[:],
                    lhsT=x_codes[m][:, cols].bitcast(FP8X4),
                    lhsT_scale=x_scales[m][:, cols],
                    rhs=codes[:, g, :].bitcast(FP4X4),
                    rhs_scale=plane[:, g, :],
                    start=(g == 0),
                    stop=(g == passes - 1),
                )
            result = work.tile([P, GROUP], F32, name=name, bufs=4)
            for j in range(parts):
                cols = slice(j * GROUP // parts, (j + 1) * GROUP // parts)
                nc.scalar.activation(out=result[:, cols], in_=acc[:, cols], func=TANH)
            return result

        def question_side(i):
            n = CHUNKS[i][1]
            tanh_q[i] = project(i, wq[n], sq[n], 0, GQ, "tanh_q", 1)

        def image_side(i, parts=1):
            n = CHUNKS[i][1]
            tanh_v[i] = project(i, wv[n], sv[n], GQ, GV, "tanh_v", parts)

        def apply_gain(i):
            gained[i] = work.tile([P, GROUP], F32, name="gained", bufs=4)
            nc.vector.tensor_tensor(out=gained[i][:], in0=tanh_q[i][:], in1=gain[:, columns(CHUNKS[i][1])], op=MULT)

        def product(i):
            m, n = CHUNKS[i]
            y32[i] = work.tile([P, GROUP], F32, name="y32", bufs=8)
            nc.vector.tensor_tensor(out=y32[i][:], in0=gained[i][:], in1=tanh_v[i][:], op=MULT)
            nc.sync.dma_start(out=out_0[m * P : (m + 1) * P, columns(n)], in_=y32[i][:])


        def by_word_parity(ap):
            return ap.rearrange("p (q u e) -> p u q e", u=2, e=2)

        def new_y16(i):
            y16[i] = work.tile([P, GROUP], BF16, name="y16", bufs=6, align_bytes=64)
            return y16[i][:].rearrange("p (u q e) -> p u q e", u=2, e=2)

        def round_y(i, copy):
            copy(out=new_y16(i), in_=by_word_parity(y32[i][:]))

        def turn_y(ids):
            bank = next_bank("turn", TURN_BANKS, [P, 4, P])
            for c, i in enumerate(ids):
                words = y16[i][:].bitcast(F32)
                for u in range(2):
                    nc.tensor.transpose(bank[:, 2 * c + u, :], words[:, u * P : (u + 1) * P], ident[:])
            return bank

        def drain_y(ids, bank):
            turned = work.tile([P, 2 * GROUP], BF16, name="y_turned", bufs=4, align_bytes=64)
            copy_out(turned[:, : len(ids) * GROUP], bank, len(ids), nc.scalar.copy)
            return turned

        chunks_left = [(b - a) * N_TILES for a, b in STORE_RANGES]

        def quantize_y(ids, turned):
            for c, i in enumerate(ids):
                m, n = CHUNKS[i]
                k = [j for j, (a, b) in enumerate(STORE_RANGES) if a <= m < b][0]
                cols = slice((m - STORE_RANGES[k][0]) * P, (m - STORE_RANGES[k][0] + 1) * P)
                nc.vector.quantize_mx(
                    out=y_codes[k][:, n, cols].bitcast(FP8X4), scales=y_scales[k][:, n, cols], in_=turned[:, columns(c)]
                )
                chunks_left[k] = chunks_left[k] - 1
                if chunks_left[k] == 0 and k < len(STORE_RANGES) - 1:
                    store_codes(k, slice(0, N_TILES))
                    store_scales(k, [nc.sync] * 4)


        load_question(0)
        load_question(1)
        nc.sync.dma_start(out=gain_rows[:], in_=joint_gain.rearrange("(j p e) -> p j e", p=P, e=4))
        nc.vector.memset(warm_in[:], 0.0)
        nc.scalar.activation(out=warm_out[:], in_=warm_in[:], func=TANH)
        make_identity(nc, ident[:])
        for n in range(N_TILES):
            for plane in (sq[n], sv[n]):
                nc.vector.memset(plane[:].rearrange("p g n -> p (g n)").bitcast(I32), 0)
        for n in range(N_TILES):
            load_weights(wq[n], sq[n], wq_words, wq_scales, n)
            if n == 0:
                load_image(0)
                load_image(1)
            load_weights(wv[n], sv[n], wv_words, wv_scales, n)
            if n > 0:
                load_rows(n + 1)
        load_rows(4)

        prepare_x(0, QUESTION)
        prepare_x(1, QUESTION)
        gain_words = gain_rows[:].bitcast(F32)
        for tiles in ([0, 1], [2]):
            bank = next_bank("turn", TURN_BANKS, [P, 4, P])
            for c, n in enumerate(tiles):
                for u in range(2):
                    nc.tensor.transpose(bank[:, 2 * c + u, :], gain_words[:, n, u : u + 1].to_broadcast([P, P]), ident[:])
            copy_out(gain[:, tiles[0] * GROUP : (tiles[-1] + 1) * GROUP], bank, len(tiles), nc.vector.tensor_copy)

        question_side(0)
        prepare_x(0, IMAGE_LO)
        prepare_x(0, IMAGE_HI)
        apply_gain(0)
        prepare_x(1, IMAGE_LO)
        prepare_x(1, IMAGE_HI)
        question_side(1)
        image_side(0)
        apply_gain(1)
        product(0)
        image_side(1)
        round_y(0, nc.vector.tensor_copy)
        product(1)
        question_side(2)
        apply_gain(2)
        round_y(1, nc.vector.tensor_copy)
        image_side(2)
        product(2)


        for i in range(N_TILES, len(CHUNKS) - N_TILES, N_TILES):
            turning = i // N_TILES + 1
            question_side(i)
            apply_gain(i)
            round_y(i - 1, nc.vector.tensor_copy)
            image_side(i)
            if turning + 3 < M_TILES:
                load_rows(turning + 3)
            turned_question = turn_x(turning, QUESTION)
            if 3 < turning + 1 < M_TILES:
                sort_words(turning + 1, IMAGE_LO, nc.vector.tensor_copy)
            pair, single = [i - 3, i - 2], [i - 1]
            turned_pair = drain_y(pair, turn_y(pair))
            product(i)
            quantize_x(turning, QUESTION, turned_question)
            turned_lo = turn_x(turning, IMAGE_LO)
            turned_hi = turn_x(turning, IMAGE_HI)
            bank = turn_y(single)
            quantize_x(turning, IMAGE_LO, turned_lo)
            quantize_y(pair, turned_pair)

            question_side(i + 1)
            turned_single = drain_y(single, bank)
            round_y(i, nc.vector.tensor_copy)
            apply_gain(i + 1)
            image_side(i + 1)
            quantize_x(turning, IMAGE_HI, turned_hi)
            product(i + 1)

            question_side(i + 2)
            if turning + 1 < M_TILES:
                sort_words(turning + 1, QUESTION, nc.scalar.copy)
            apply_gain(i + 2)
            round_y(i + 1, nc.vector.tensor_copy)
            image_side(i + 2)
            product(i + 2)
            quantize_y(single, turned_single)


        i = len(CHUNKS) - N_TILES
        question_side(i)
        question_side(i + 1)
        round_y(i - 1, nc.vector.tensor_copy)
        apply_gain(i)
        apply_gain(i + 1)
        image_side(i)
        pair, single = [i - 3, i - 2], [i - 1]
        pair_bank = turn_y(pair)
        single_bank = turn_y(single)
        product(i)
        turned_pair = drain_y(pair, pair_bank)
        turned_single = drain_y(single, single_bank)
        quantize_y(pair, turned_pair)
        image_side(i + 1)
        question_side(i + 2)
        round_y(i, nc.scalar.copy)
        quantize_y(single, turned_single)
        product(i + 1)
        apply_gain(i + 2)
        image_side(i + 2, 2)
        round_y(i + 1, nc.vector.tensor_copy)
        rounded = new_y16(i + 2)
        for half in range(2):
            cols = slice(half * GROUP // 2, (half + 1) * GROUP // 2)
            nc.vector.tensor_tensor(
                out=rounded[:, :, half * P // 2 : (half + 1) * P // 2, :],
                in0=by_word_parity(gained[i + 2][:, cols]),
                in1=by_word_parity(tanh_v[i + 2][:, cols]),
                op=MULT,
            )
        product(i + 2)
        pair, single = [i, i + 1], [i + 2]
        pair_bank = turn_y(pair)
        single_bank = turn_y(single)
        turned_pair = drain_y(pair, pair_bank)
        turned_single = drain_y(single, single_bank)
        last_range = len(STORE_RANGES) - 1
        quantize_y(pair, turned_pair)
        store_codes(last_range, slice(0, 2))
        quantize_y(single, turned_single)
        store_codes(last_range, slice(2, 3))
        store_scales(last_range, [nc.scalar, nc.sync, nc.scalar, nc.sync])
